import numpy as np
import ml_dtypes


def mxq(x, axis, fmt="e4m3"):
    dtype, down = {"e4m3": (ml_dtypes.float8_e4m3fn, 7), "e5m2": (ml_dtypes.float8_e5m2, 14)}[fmt]
    v = np.moveaxis(np.asarray(x, np.float32).astype(ml_dtypes.bfloat16).astype(np.float64), axis, -1)
    blocks = v.reshape(v.shape[:-1] + (-1, 32))
    amax = np.abs(blocks).max(-1, keepdims=True)
    byte = np.maximum(np.where(amax > 0, np.frexp(amax)[1] - 1 + 127, 0) - down, 1)
    scale = np.exp2(byte - 127.0)
    codes = (blocks / scale).astype(np.float32).astype(dtype).astype(np.float64)
    return np.moveaxis((codes * scale).reshape(v.shape), -1, axis)


WIDE = False


def mx_kscale(k):
    if not WIDE:
        return np.ones(k)
    levels = np.array([10, -10, 5, -5, 0])
    if k % 512:
        return np.exp2(np.random.permutation(np.resize(levels, k // 32))).repeat(32)
    a = np.empty((k // 512, 16))
    for p in range(k // 512):
        a[p, :8] = np.random.permutation(np.resize(levels, 8))
        for g in range(8):
            far = levels[np.abs(levels - a[p, g]) >= 10]
            a[p, g + 8] = far[np.random.randint(len(far))]
    return np.exp2(a.ravel()).repeat(32)


def f64(x):
    return np.asarray(x).astype(np.float64)


def striped(idx):
    return np.tile(idx.reshape(-1, 16).T, (8, 1)).astype(np.uint16)


def unstriped(offs):
    return offs[:16].T.reshape(-1).astype(np.int64)


E2M1 = np.array([0.0, 0.5, 1.0, 1.5, 2.0, 3.0, 4.0, 6.0, -0.0, -0.5, -1.0, -1.5, -2.0, -3.0, -4.0, -6.0])


def pack_weight(w, fmt):
    k, n = w.shape
    w = f64(np.asarray(w, np.float32).astype(ml_dtypes.bfloat16)).reshape(k // 32, 32, n)
    amax = np.abs(w).max(1)
    if fmt == "e4m3":
        byte = np.frexp(amax)[1] - 1 + 127 - 7
    else:
        mant, ex = np.frexp(amax / 6.0)
        byte = np.where(mant > 0.5, ex, ex - 1) + 127
    byte = np.clip(np.where(amax > 0, byte, 1), 1, 254)
    scaled = (w * np.exp2(127.0 - byte)[:, None, :]).reshape(k, n).astype(np.float32)
    by_word = np.ascontiguousarray(scaled.reshape(k // 512, 128, 4, n).transpose(0, 1, 3, 2))
    if fmt == "e4m3":
        words = by_word.astype(ml_dtypes.float8_e4m3fn).view(np.uint8)
    else:
        c = by_word.astype(ml_dtypes.float4_e2m1fn).view(np.uint8) & 0xF
        words = (c[..., 0::2] | (c[..., 1::2] << 4)).reshape(k // 512, 128, 2 * n)
    return np.ascontiguousarray(words), np.ascontiguousarray(byte.astype(np.uint8).reshape(k // 512, 16, n))


def unpack_weight(words, scales, fmt):
    g, _, n = scales.shape
    words = np.ascontiguousarray(words).reshape(g, 128, n, -1)
    if fmt == "e4m3":
        vals = words.view(ml_dtypes.float8_e4m3fn).astype(np.float64)
    else:
        nib = np.empty((g, 128, n, 4), np.uint8)
        nib[..., 0::2] = words & 0xF
        nib[..., 1::2] = words >> 4
        vals = E2M1[nib]
    vals = vals * np.repeat(np.exp2(scales.astype(np.float64) - 127.0), 8, axis=1)[..., None]
    return vals.transpose(0, 1, 3, 2).reshape(g * 512, n)


def gelu(v):
    return 0.5 * v * (1.0 + np.tanh(np.sqrt(2.0 / np.pi) * (v + 0.044715 * v**3)))


K, K2, T, T2, S, P, H, N = 1024, 512, 4096, 2048, 1024, 512, 1024, 512


def setup_inputs():
    n = np.random.standard_normal
    s = mx_kscale(K)[:, None]
    s2 = mx_kscale(K2)[:, None]
    u = mx_kscale(H)[:, None]
    d = {}
    d["tab_words"], d["tab_scales"] = pack_weight(n((K, T)) * s, "e4m3")
    d["offs"] = striped(np.random.permutation(T)[:S])
    d["tab2_words"], d["tab2_scales"] = pack_weight(n((K2, T2)) * s2, "e4m3")
    d["offs2"] = striped(np.random.permutation(T2)[:P])
    d["pos1"] = striped(np.random.permutation(S)[:P])
    d["w1"] = (0.56 * n((K, H)) / s / K ** 0.5).astype(np.float32)
    d["ga"] = (2.0 * np.exp(0.3 * n(H)) * u[:, 0]).astype(np.float32)
    d["w2_words"], d["w2_scales"] = pack_weight(n((K2, H)) / s2 * u.T / K2 ** 0.5, "e2m1")
    d["grain"] = (0.8 * n((H, P)) * u).astype(np.float32)
    d["wgs"] = np.exp(0.3 * n((128, P))).astype(np.float32)
    d["w3_words"], d["w3_scales"] = pack_weight(1.8 * n((H, N)) / u / H ** 0.5, "e4m3")
    return d


def reference(tab_words, tab_scales, offs, tab2_words, tab2_scales, offs2, pos1,
              w1, ga, w2_words, w2_scales, grain, wgs, w3_words, w3_scales):
    v = unpack_weight(tab_words, tab_scales, "e4m3")[:, unstriped(offs)]
    v2 = unpack_weight(tab2_words, tab2_scales, "e4m3")[:, unstriped(offs2)]
    a = np.sin(mxq(f64(w1), 0, "e4m3").T @ v) * f64(ga)[:, None]
    b = (unpack_weight(w2_words, w2_scales, "e2m1").T @ v2) + f64(grain)
    placed = np.zeros((H, S))
    placed[:, unstriped(pos1)] = np.tile(f64(wgs), (H // 128, 1)) * b
    z = np.maximum(a, placed)
    y = unpack_weight(w3_words, w3_scales, "e4m3").T @ mxq(z, 0, "e4m3")
    return np.sqrt(1.0 + np.square(y))

@@ -1,0 +1,287 @@
+import math
+from contextlib import ExitStack
+
+import concourse.mybir as mybir
+
+K, K2, T, T2, S, SP, H, N = 1024, 512, 4096, 2048, 1024, 512, 1024, 512
+FLOPS = 2 * (K * H * S + K2 * H * SP + H * N * S)
+
+F32 = mybir.dt.float32
+BF16 = mybir.dt.bfloat16
+I32 = mybir.dt.int32
+U32 = mybir.dt.uint32
+U16 = mybir.dt.uint16
+U8 = mybir.dt.uint8
+FP8X4 = mybir.dt.float8_e4m3fn_x4
+FP4X4 = mybir.dt.float4_e2m1fn_x4
+ALU = mybir.AluOpType
+ACT = mybir.ActivationFunctionType
+
+P = 128
+PACK = 4
+KP = P * PACK
+BANK = 512
+ROUND = 1.5 * 2.0**23
+X_BANKS = 6
+PIECES = ((512, 256), (768, 128), (896, 128))
+
+
+def tile_list_slate_splitting_scores_kernel(
+    tc, tab_words, tab_scales, offs, tab2_words, tab2_scales, offs2, pos1,
+    w1, ga, w2_words, w2_scales, grain, wgs, w3_words, w3_scales, out,
+):
+    nc = tc.nc
+    with ExitStack() as ctx:
+        keep = ctx.enter_context(tc.tile_pool(name="keep", bufs=1))
+        ring = ctx.enter_context(tc.tile_pool(name="ring", bufs=2))
+        psum = ctx.enter_context(tc.psum_pool(name="psum", bufs=1))
+
+        def held(name, shape, dtype):
+            return keep.tile(shape, dtype, name=name, align_bytes=64)
+
+        banks = [psum.tile([P, BANK], F32, name="bank%d" % i) for i in range(8)]
+
+        offs_t = keep.tile([P, S // 16], U16, name="offs_t")
+        offs2_t = keep.tile([P, SP // 16], U16, name="offs2_t")
+        pos_t = keep.tile([P, SP // 16], U16, name="pos_t")
+        tabw = [held("tabw%d" % a, [P, T], I32) for a in range(2)]
+        tabs = held("tabs", [P, T], U8)
+        tab2w = held("tab2w", [P, T2], I32)
+        tab2s = held("tab2s", [P, T2], U8)
+        w2w_raw = held("w2w_raw", [P, 2 * H], U8)
+        w2s_raw = held("w2s_raw", [P, H], U8)
+        w2w = held("w2w", [P, 2 * H], U8)
+        w2s = held("w2s", [P, H], U8)
+        w3w = held("w3w", [P, 2, N], I32)
+        w3s = held("w3s", [P, N], U8)
+        wg = held("wg", [P, PACK * SP], F32)
+        ga_t = held("ga_t", [P, 2, PACK], F32)
+        gr = [keep.tile([P, SP], F32, name="gr%d" % k, tag="slice%d" % (k + 1)) for k in range(8)]
+        pages = {}
+
+        def clear_page(k):
+            pages[k] = keep.tile([P, S], F32, name="page%d" % k, tag="slice%d" % k)
+            nc.gpsimd.memset(pages[k][:], 0.0)
+
+        gw = [[held("gw%d%d" % (a, h), [P, BANK], U32) for h in range(2)] for a in range(2)]
+        gs = held("gs", [P, S], U8)
+        g2w = held("g2w", [P, SP], U32)
+        g2s = held("g2s", [P, SP], U8)
+        w1c = [[held("w1c%d%d" % (a, b), [P, KP], U32) for b in range(2)] for a in range(2)]
+        w1s = [[held("w1s%d%d" % (a, b), [P, KP], U8) for b in range(2)] for a in range(2)]
+        zc = [[held("zc%d%d" % (b, h), [P, BANK], U32) for h in range(2)] for b in range(2)]
+        zs = [[held("zs%d%d" % (b, h), [P, BANK], U8) for h in range(2)] for b in range(2)]
+        one = held("one", [P, 1], F32)
+        warm = held("warm", [P, 1], F32)
+
+        def big(name):
+            return ring.tile([P, PACK, BANK], F32, name=name, tag="big", bufs=5, align_bytes=64)
+
+        nc.gpsimd.memset(w2s_raw[:].bitcast(I32), 0)
+        nc.gpsimd.memset(tab2s[:].bitcast(I32), 0)
+        nc.vector.memset(one[:], 1.0)
+        nc.scalar.activation(warm[:], one[:], ACT.Sin)
+        nc.vector.memset(tabs[:].bitcast(I32), 0)
+        nc.vector.memset(w3s[:].bitcast(I32), 0)
+        clear_page(0)
+
+        def load_words(tile_ap, words):
+            nc.sync.dma_start(tile_ap, words.rearrange("p n i -> p (n i)").bitcast(I32))
+
+        def load_scale_rows(tile, scales, a):
+            for q in range(4):
+                r0 = 32 * q + 4 * a
+                nc.sync.dma_start(tile[r0 : r0 + 4, :].bitcast(I32), scales[a, 4 * q : 4 * q + 4, :].bitcast(I32))
+
+        def load_packed_rows(tile, scales):
+            for q in range(4):
+                nc.gpsimd.dma_start(tile[32 * q : 32 * q + 8, :].bitcast(I32), scales[:, 4 * q : 4 * q + 4, :].bitcast(I32))
+
+        grain_v = grain.rearrange("(b p t) j -> b t p j", b=2, t=PACK)
+
+        def load_grain(k):
+            nc.sync.dma_start(gr[k][:], grain_v[k // PACK, k % PACK])
+
+        w1_raw = {}
+
+        def load_w1(a, b):
+            w1_raw[a, b] = big("w1_raw%d%d" % (a, b))
+            rows = w1[a * KP : (a + 1) * KP, b * KP : (b + 1) * KP]
+            nc.sync.dma_start(w1_raw[a, b][:], rows.rearrange("(p j) c -> p j c", j=PACK))
+
+        nc.sync.dma_start(offs2_t[:], offs2)
+        nc.sync.dma_start(w2w_raw[:].bitcast(I32), w2_words[0].bitcast(I32))
+        nc.sync.dma_start(pos_t[:], pos1)
+        load_scale_rows(w2s_raw, w2_scales, 0)
+        load_words(tab2w[:], tab2_words[0])
+        load_scale_rows(tab2s, tab2_scales, 0)
+        load_grain(0)
+        wgs_v = wgs.rearrange("(m t) j -> m (t j)", t=PACK)
+        for q in (0, 2, 1, 3):
+            nc.sync.dma_start(wg[32 * q : 32 * q + 32, :], wgs_v)
+        load_grain(1)
+        load_words(tabw[0][:], tab_words[0])
+        nc.sync.dma_start(offs_t[:], offs)
+        load_packed_rows(tabs, tab_scales)
+        load_w1(0, 0)
+        load_w1(1, 0)
+        load_words(tabw[1][:], tab_words[1])
+        load_grain(2)
+        load_w1(0, 1)
+        load_grain(3)
+        load_w1(1, 1)
+        nc.sync.dma_start(ga_t[:], ga.rearrange("(b p t) -> p b t", b=2, t=PACK))
+        for k in range(4, 8):
+            load_grain(k)
+        nc.sync.dma_start(w3w[:], w3_words.rearrange("a p n i -> p a (n i)").bitcast(I32))
+        load_packed_rows(w3s, w3_scales)
+
+        nc.vector.tensor_copy(
+            w2w[:].rearrange("p (b t m e) -> p b t m e", b=2, t=PACK, e=2),
+            w2w_raw[:].rearrange("p (b m t e) -> p b t m e", b=2, t=PACK, e=2),
+        )
+        nc.vector.tensor_copy(
+            w2s[:].rearrange("p (b t m) -> p b t m", b=2, t=PACK),
+            w2s_raw[:].rearrange("p (b m t) -> p b t m", b=2, t=PACK),
+        )
+        nc.vector.tensor_copy(g2w[:], tab2w[:].bitcast(U32).indirect(offs2_t[:]))
+        nc.vector.tensor_copy(g2s[:], tab2s[:].indirect(offs2_t[:]))
+
+        def place(k, bank):
+            c0 = P * k
+            nc.tensor.matmul_mx(
+                bank[:], lhsT=w2w[:, 2 * c0 : 2 * c0 + 2 * P].bitcast(FP4X4), lhsT_scale=w2s[:, c0 : c0 + P],
+                rhs=g2w[:].bitcast(FP8X4), rhs_scale=g2s[:], start=True, stop=True,
+            )
+            bsum = ring.tile([P, SP], F32, name="bsum", tag="bsum")
+            nc.vector.tensor_tensor(bsum[:], bank[:], gr[k][:], ALU.add)
+            if k + 1 < 8:
+                clear_page(k + 1)
+            t = k % PACK
+            nc.vector.tensor_tensor(pages[k][:].indirect(pos_t[:]), bsum[:], wg[:, t * SP : (t + 1) * SP], ALU.mult)
+
+        def quantise_w1(a, b):
+            w1_bf = ring.tile([P, PACK * KP], BF16, name="w1_bf", tag="w1_bf", align_bytes=64)
+            nc.scalar.copy(
+                w1_bf[:].rearrange("p (t m j) -> p m j t", t=PACK, j=PACK),
+                w1_raw[a, b][:].rearrange("p j (m t) -> p m j t", t=PACK),
+            )
+            nc.vector.quantize_mx(w1c[a][b][:].bitcast(FP8X4), w1s[a][b][:], w1_bf[:])
+
+        def gather_words(a, h):
+            part = offs_t[:, h * (BANK // 16) : (h + 1) * (BANK // 16)]
+            nc.vector.tensor_copy(gw[a][h][:], tabw[a][:].bitcast(U32).indirect(part))
+
+        place(0, banks[6])
+        place(1, banks[7])
+        gather_words(0, 0)
+        nc.vector.tensor_copy(gs[:], tabs[:].indirect(offs_t[:]))
+        quantise_w1(0, 0)
+        gather_words(0, 1)
+        quantise_w1(1, 0)
+        gather_words(1, 0)
+        gather_words(1, 1)
+        place(2, banks[6])
+
+        turns = {}
+
+        def angle(i):
+            h, b, t = i // 8, i // 4 % 2, i % 4
+            if t == 0:
+                turns[b, h] = big("turns%d%d" % (b, h))
+            bank = banks[i % X_BANKS]
+            for a in range(2):
+                nc.tensor.matmul_mx(
+                    bank[:], lhsT=w1c[a][b][:, t * P : (t + 1) * P].bitcast(FP8X4),
+                    lhsT_scale=w1s[a][b][:, t * P : (t + 1) * P],
+                    rhs=gw[a][h][:].bitcast(FP8X4), rhs_scale=gs[4 * a : P, h * BANK : (h + 1) * BANK],
+                    start=(a == 0), stop=(a == 1),
+                )
+            whole = ring.tile([P, BANK], U32, name="whole", tag="whole", bufs=9)
+            x = turns[b, h][:, t, :]
+            nc.scalar.activation(x, bank[:], ACT.Copy, scale=0.5 / math.pi)
+            nc.scalar.activation(whole[:], bank[:], ACT.Copy, scale=0.5 / math.pi, bias=ROUND)
+            nc.vector.scalar_tensor_tensor(x, whole[:].bitcast(I32), ROUND, x, ALU.subtract, ALU.subtract)
+
+        def sine(i):
+            h, b, t = i // 8, i // 4 % 2, i % 4
+            x = turns[b, h][:, t, :]
+            nc.scalar.activation(x, x, ACT.Sin, scale=-2.0 * math.pi)
+
+        def join(b, c0, width, engine):
+            h, lo = divmod(c0, BANK)
+            planar = ring.tile([P, PACK, width], BF16, name="planar", tag="planar%d" % width, bufs=1 if width == BANK else 2, align_bytes=64)
+            for t in range(PACK):
+                nc.vector.scalar_tensor_tensor(
+                    planar[:, t, :], turns[b, h][:, t, lo : lo + width], ga_t[:, b, t : t + 1],
+                    pages[PACK * b + t][:, c0 : c0 + width], ALU.mult, ALU.max,
+                )
+            woven = ring.tile([P, width * PACK], BF16, name="woven", tag="woven", align_bytes=64)
+            dst = woven[:].rearrange("p (c i t) -> p c t i", i=4, t=PACK)
+            src = planar[:].rearrange("p t (c i) -> p c t i", i=4)
+            if engine == "scalar":
+                nc.scalar.copy(dst, src)
+            else:
+                nc.vector.tensor_copy(dst, src)
+            nc.vector.quantize_mx(zc[b][h][:, lo : lo + width].bitcast(FP8X4), zs[b][h][:, lo : lo + width], woven[:])
+
+        out_v = out.rearrange("(n p) j -> p n j", p=P)
+
+        def squares(c0, width, first_bank):
+            h, lo = divmod(c0, BANK)
+            per_bank = BANK // width
+            scores = []
+            for g in range(4 // per_bank):
+                bank = banks[(first_bank + g) % 8]
+                for n in range(per_bank):
+                    n0 = (g * per_bank + n) * P
+                    for b in range(2):
+                        nc.tensor.matmul_mx(
+                            bank[:, n * width : (n + 1) * width], lhsT=w3w[:, b, n0 : n0 + P].bitcast(FP8X4),
+                            lhsT_scale=w3s[4 * b : P, n0 : n0 + P],
+                            rhs=zc[b][h][:, lo : lo + width].bitcast(FP8X4), rhs_scale=zs[b][h][:, lo : lo + width],
+                            start=(b == 0), stop=(b == 1),
+                        )
+                score = ring.tile([P, BANK], F32, name="score", tag="score", bufs=8)
+                nc.scalar.activation(score[:], bank[:], ACT.Square)
+                scores.append(score)
+            return scores
+
+        def roots(c0, width, scores):
+            per_bank = BANK // width
+            for g, score in enumerate(scores):
+                nc.scalar.activation(score[:], score[:], ACT.Sqrt, bias=one[:])
+                nc.sync.dma_start(
+                    out_v[:, g * per_bank : (g + 1) * per_bank, c0 : c0 + width],
+                    score[:].rearrange("p (n j) -> p n j", n=per_bank),
+                )
+
+        def angles(g, placed_after):
+            for i in range(4 * g, 4 * g + 4):
+                angle(i)
+                if i in placed_after:
+                    place(placed_after[i], banks[i % X_BANKS])
+
+        def sines(g):
+            for i in range(4 * g, 4 * g + 4):
+                sine(i)
+
+        angles(0, {1: 3})
+        quantise_w1(0, 1)
+        quantise_w1(1, 1)
+        sines(0)
+        angles(1, {4: 4, 5: 5, 6: 6, 7: 7})
+        join(0, 0, BANK, "scalar")
+        angles(2, {})
+        sines(1)
+        angles(3, {})
+        sines(2)
+        join(1, 0, BANK, "scalar")
+        sines(3)
+        join(0, BANK, BANK, "vector")
+        roots(0, BANK, squares(0, BANK, 6))
+        first_bank = 2
+        for c0, width in PIECES:
+            join(1, c0, width, "vector")
+            roots(c0, width, squares(c0, width, first_bank))
+            first_bank += 4 * width // BANK

@@ -2,6 +2,7 @@ import math
 from contextlib import ExitStack
 
 import concourse.mybir as mybir
+from concourse.masks import make_identity
 
 K, K2, T, T2, S, SP, H, N = 1024, 512, 4096, 2048, 1024, 512, 1024, 512
 FLOPS = 2 * (K * H * S + K2 * H * SP + H * N * S)
@@ -22,7 +23,6 @@ PACK = 4
 KP = P * PACK
 BANK = 512
 ROUND = 1.5 * 2.0**23
-X_BANKS = 6
 PIECES = ((512, 256), (768, 128), (896, 128))
 
 
@@ -56,12 +56,12 @@ def tile_list_slate_splitting_scores_kernel(
         w3s = held("w3s", [P, N], U8)
         wg = held("wg", [P, PACK * SP], F32)
         ga_t = held("ga_t", [P, 2, PACK], F32)
-        gr = [keep.tile([P, SP], F32, name="gr%d" % k, tag="slice%d" % (k + 1)) for k in range(8)]
+        gr = [keep.tile([P, SP], F32, name="gr%d" % k, tag="slice%d" % (k + 1 if k >= 3 else -k - 1)) for k in range(8)]
         pages = {}
 
         def clear_page(k):
             pages[k] = keep.tile([P, S], F32, name="page%d" % k, tag="slice%d" % k)
-            nc.gpsimd.memset(pages[k][:], 0.0)
+            nc.vector.memset(pages[k][:].bitcast(I32), 0)
 
         gw = [[held("gw%d%d" % (a, h), [P, BANK], U32) for h in range(2)] for a in range(2)]
         gs = held("gs", [P, S], U8)
@@ -83,7 +83,11 @@ def tile_list_slate_splitting_scores_kernel(
         nc.scalar.activation(warm[:], one[:], ACT.Sin)
         nc.vector.memset(tabs[:].bitcast(I32), 0)
         nc.vector.memset(w3s[:].bitcast(I32), 0)
-        clear_page(0)
+        for k in range(4):
+            clear_page(k)
+
+        ident = held("ident", [P, P], F32)
+        make_identity(nc, ident[:])
 
         def load_words(tile_ap, words):
             nc.sync.dma_start(tile_ap, words.rearrange("p n i -> p (n i)").bitcast(I32))
@@ -95,7 +99,7 @@ def tile_list_slate_splitting_scores_kernel(
 
         def load_packed_rows(tile, scales):
             for q in range(4):
-                nc.gpsimd.dma_start(tile[32 * q : 32 * q + 8, :].bitcast(I32), scales[:, 4 * q : 4 * q + 4, :].bitcast(I32))
+                nc.sync.dma_start(tile[32 * q : 32 * q + 8, :].bitcast(I32), scales[:, 4 * q : 4 * q + 4, :].bitcast(I32))
 
         grain_v = grain.rearrange("(b p t) j -> b t p j", b=2, t=PACK)
 
@@ -121,8 +125,8 @@ def tile_list_slate_splitting_scores_kernel(
             nc.sync.dma_start(wg[32 * q : 32 * q + 32, :], wgs_v)
         load_grain(1)
         load_words(tabw[0][:], tab_words[0])
-        nc.sync.dma_start(offs_t[:], offs)
         load_packed_rows(tabs, tab_scales)
+        nc.sync.dma_start(offs_t[:], offs)
         load_w1(0, 0)
         load_w1(1, 0)
         load_words(tabw[1][:], tab_words[1])
@@ -137,8 +141,8 @@ def tile_list_slate_splitting_scores_kernel(
         load_packed_rows(w3s, w3_scales)
 
         nc.vector.tensor_copy(
-            w2w[:].rearrange("p (b t m e) -> p b t m e", b=2, t=PACK, e=2),
-            w2w_raw[:].rearrange("p (b m t e) -> p b t m e", b=2, t=PACK, e=2),
+            w2w[:].bitcast(U16).rearrange("p (b t m) -> p b t m", b=2, t=PACK),
+            w2w_raw[:].bitcast(U16).rearrange("p (b m t) -> p b t m", b=2, t=PACK),
         )
         nc.vector.tensor_copy(
             w2s[:].rearrange("p (b t m) -> p b t m", b=2, t=PACK),
@@ -147,21 +151,33 @@ def tile_list_slate_splitting_scores_kernel(
         nc.vector.tensor_copy(g2w[:], tab2w[:].bitcast(U32).indirect(offs2_t[:]))
         nc.vector.tensor_copy(g2s[:], tab2s[:].indirect(offs2_t[:]))
 
-        def place(k, bank):
+        unit_bank = [banks[i] for i in (6, 7, 6, 7, 0, 1, 4, 5)]
+        late = {8: 4, 9: 5, 6: 6, 7: 7}
+
+        def whole_tile(i):
+            if i in late:
+                return keep.tile([P, BANK], U32, name="whole", tag="late%d" % late[i])
+            return ring.tile([P, BANK], U32, name="whole", tag="whole", bufs=4)
+
+        def place(k):
             c0 = P * k
+            bank = unit_bank[k]
             nc.tensor.matmul_mx(
                 bank[:], lhsT=w2w[:, 2 * c0 : 2 * c0 + 2 * P].bitcast(FP4X4), lhsT_scale=w2s[:, c0 : c0 + P],
                 rhs=g2w[:].bitcast(FP8X4), rhs_scale=g2s[:], start=True, stop=True,
             )
-            bsum = ring.tile([P, SP], F32, name="bsum", tag="bsum")
+            if k < 4:
+                bsum = ring.tile([P, SP], F32, name="bsum", tag="bsum")
+            else:
+                bsum = keep.tile([P, SP], F32, name="bsum", tag="late%d" % k)
             nc.vector.tensor_tensor(bsum[:], bank[:], gr[k][:], ALU.add)
-            if k + 1 < 8:
+            if 4 <= k + 1 < 8:
                 clear_page(k + 1)
             t = k % PACK
             nc.vector.tensor_tensor(pages[k][:].indirect(pos_t[:]), bsum[:], wg[:, t * SP : (t + 1) * SP], ALU.mult)
 
         def quantise_w1(a, b):
-            w1_bf = ring.tile([P, PACK * KP], BF16, name="w1_bf", tag="w1_bf", align_bytes=64)
+            w1_bf = ring.tile([P, PACK * KP], BF16, name="w1_bf", tag="woven512", align_bytes=64)
             nc.scalar.copy(
                 w1_bf[:].rearrange("p (t m j) -> p m j t", t=PACK, j=PACK),
                 w1_raw[a, b][:].rearrange("p j (m t) -> p m j t", t=PACK),
@@ -172,8 +188,8 @@ def tile_list_slate_splitting_scores_kernel(
             part = offs_t[:, h * (BANK // 16) : (h + 1) * (BANK // 16)]
             nc.vector.tensor_copy(gw[a][h][:], tabw[a][:].bitcast(U32).indirect(part))
 
-        place(0, banks[6])
-        place(1, banks[7])
+        place(0)
+        place(1)
         gather_words(0, 0)
         nc.vector.tensor_copy(gs[:], tabs[:].indirect(offs_t[:]))
         quantise_w1(0, 0)
@@ -181,15 +197,16 @@ def tile_list_slate_splitting_scores_kernel(
         quantise_w1(1, 0)
         gather_words(1, 0)
         gather_words(1, 1)
-        place(2, banks[6])
+        place(2)
 
         turns = {}
+        wholes = {}
 
         def angle(i):
             h, b, t = i // 8, i // 4 % 2, i % 4
             if t == 0:
                 turns[b, h] = big("turns%d%d" % (b, h))
-            bank = banks[i % X_BANKS]
+            bank = banks[2 + i % 2]
             for a in range(2):
                 nc.tensor.matmul_mx(
                     bank[:], lhsT=w1c[a][b][:, t * P : (t + 1) * P].bitcast(FP8X4),
@@ -197,18 +214,57 @@ def tile_list_slate_splitting_scores_kernel(
                     rhs=gw[a][h][:].bitcast(FP8X4), rhs_scale=gs[4 * a : P, h * BANK : (h + 1) * BANK],
                     start=(a == 0), stop=(a == 1),
                 )
-            whole = ring.tile([P, BANK], U32, name="whole", tag="whole", bufs=9)
+            whole = whole_tile(i)
             x = turns[b, h][:, t, :]
             nc.scalar.activation(x, bank[:], ACT.Copy, scale=0.5 / math.pi)
             nc.scalar.activation(whole[:], bank[:], ACT.Copy, scale=0.5 / math.pi, bias=ROUND)
-            nc.vector.scalar_tensor_tensor(x, whole[:].bitcast(I32), ROUND, x, ALU.subtract, ALU.subtract)
+            wholes[i] = whole
+
+        def wrap(i):
+            h, b, t = i // 8, i // 4 % 2, i % 4
+            x = turns[b, h][:, t, :]
+            nc.vector.scalar_tensor_tensor(x, wholes[i][:].bitcast(I32), ROUND, x, ALU.subtract, ALU.subtract)
+
+        parts = {}
+
+        def angle_turned(i):
+            b, jt = i // 4 % 2, i % 4
+            if jt == 0:
+                turns[b, 1] = big("turns%d1" % b)
+            bank = banks[2 + i % 2]
+            for a in range(2):
+                nc.tensor.matmul_mx(
+                    bank[:], lhsT=gw[a][1][:, jt * P : (jt + 1) * P].bitcast(FP8X4),
+                    lhsT_scale=gs[4 * a : P, BANK + jt * P : BANK + (jt + 1) * P],
+                    rhs=w1c[a][b][:].bitcast(FP8X4), rhs_scale=w1s[a][b][:],
+                    start=(a == 0), stop=(a == 1),
+                )
+            whole = whole_tile(i)
+            full = ring.tile([P, BANK], F32, name="full", tag="full", bufs=2)
+            minus = ring.tile([P, BANK], F32, name="minus", tag="minus", bufs=2)
+            nc.scalar.activation(whole[:], bank[:], ACT.Copy, scale=0.5 / math.pi, bias=ROUND)
+            nc.scalar.activation(full[:], bank[:], ACT.Copy, scale=0.5 / math.pi)
+            nc.scalar.activation(minus[:], whole[:], ACT.Copy, scale=-1.0, bias=ROUND)
+            back = banks[6 + i % 2]
+            for t in range(PACK):
+                cols = slice(t * P, (t + 1) * P)
+                nc.tensor.matmul(back[:, cols], lhsT=full[:, cols], rhs=ident[:], start=True, stop=False, is_transpose=True)
+                nc.tensor.matmul(back[:, cols], lhsT=minus[:, cols], rhs=ident[:], start=False, stop=True, is_transpose=True)
+            parts[i] = back
+
+        def sine_turned(i):
+            b, jt = i // 4 % 2, i % 4
+            nc.scalar.activation(
+                turns[b, 1][:, :, jt * P : (jt + 1) * P], parts[i][:].rearrange("p (t j) -> p t j", t=PACK),
+                ACT.Sin, scale=2.0 * math.pi,
+            )
 
         def sine(i):
             h, b, t = i // 8, i // 4 % 2, i % 4
-            x = turns[b, h][:, t, :]
+            x = turns[b, h][:, t : t + 2, :]
             nc.scalar.activation(x, x, ACT.Sin, scale=-2.0 * math.pi)
 
-        def join(b, c0, width, engine):
+        def maxima(b, c0, width):
             h, lo = divmod(c0, BANK)
             planar = ring.tile([P, PACK, width], BF16, name="planar", tag="planar%d" % width, bufs=1 if width == BANK else 2, align_bytes=64)
             for t in range(PACK):
@@ -216,7 +272,11 @@ def tile_list_slate_splitting_scores_kernel(
                     planar[:, t, :], turns[b, h][:, t, lo : lo + width], ga_t[:, b, t : t + 1],
                     pages[PACK * b + t][:, c0 : c0 + width], ALU.mult, ALU.max,
                 )
-            woven = ring.tile([P, width * PACK], BF16, name="woven", tag="woven", align_bytes=64)
+            return planar
+
+        def weave(b, c0, width, planar, engine):
+            h, lo = divmod(c0, BANK)
+            woven = ring.tile([P, width * PACK], BF16, name="woven", tag="woven%d" % width, align_bytes=64)
             dst = woven[:].rearrange("p (c i t) -> p c t i", i=4, t=PACK)
             src = planar[:].rearrange("p t (c i) -> p c t i", i=4)
             if engine == "scalar":
@@ -227,61 +287,70 @@ def tile_list_slate_splitting_scores_kernel(
 
         out_v = out.rearrange("(n p) j -> p n j", p=P)
 
-        def squares(c0, width, first_bank):
+        def finish(c0, width, free_banks, score):
             h, lo = divmod(c0, BANK)
             per_bank = BANK // width
-            scores = []
-            for g in range(4 // per_bank):
-                bank = banks[(first_bank + g) % 8]
+            n_banks = 4 // per_bank
+            for g in range(n_banks):
+                bank = free_banks[g % len(free_banks)]
                 for n in range(per_bank):
                     n0 = (g * per_bank + n) * P
-                    for b in range(2):
+                    for b in (1, 0):
                         nc.tensor.matmul_mx(
                             bank[:, n * width : (n + 1) * width], lhsT=w3w[:, b, n0 : n0 + P].bitcast(FP8X4),
                             lhsT_scale=w3s[4 * b : P, n0 : n0 + P],
                             rhs=zc[b][h][:, lo : lo + width].bitcast(FP8X4), rhs_scale=zs[b][h][:, lo : lo + width],
-                            start=(b == 0), stop=(b == 1),
+                            start=(b == 1), stop=(b == 0),
                         )
-                score = ring.tile([P, BANK], F32, name="score", tag="score", bufs=8)
-                nc.scalar.activation(score[:], bank[:], ACT.Square)
-                scores.append(score)
-            return scores
-
-        def roots(c0, width, scores):
-            per_bank = BANK // width
-            for g, score in enumerate(scores):
-                nc.scalar.activation(score[:], score[:], ACT.Sqrt, bias=one[:])
+                nc.scalar.activation(score[:, g * BANK : (g + 1) * BANK], bank[:], ACT.Square)
+            step = min(2, n_banks)
+            for g in range(0, n_banks, step):
+                part = score[:, g * BANK : (g + step) * BANK]
+                nc.scalar.activation(part, part, ACT.Sqrt, bias=one[:])
                 nc.sync.dma_start(
-                    out_v[:, g * per_bank : (g + 1) * per_bank, c0 : c0 + width],
-                    score[:].rearrange("p (n j) -> p n j", n=per_bank),
+                    out_v[:, g * per_bank : (g + step) * per_bank, c0 : c0 + width],
+                    part.rearrange("p (n j) -> p n j", j=width),
                 )
 
-        def angles(g, placed_after):
-            for i in range(4 * g, 4 * g + 4):
-                angle(i)
-                if i in placed_after:
-                    place(placed_after[i], banks[i % X_BANKS])
-
         def sines(g):
-            for i in range(4 * g, 4 * g + 4):
+            for i in range(4 * g, 4 * g + 4, 2):
                 sine(i)
 
-        angles(0, {1: 3})
+        def turned_group(g):
+            for i in range(4 * g, 4 * g + 5):
+                if i < 4 * g + 4:
+                    angle_turned(i)
+                if i == 14:
+                    sines(1)
+                if i > 4 * g:
+                    sine_turned(i - 1)
+
+        for i in range(4):
+            angle(i)
+            wrap(i)
+        place(3)
         quantise_w1(0, 1)
         quantise_w1(1, 1)
         sines(0)
-        angles(1, {4: 4, 5: 5, 6: 6, 7: 7})
-        join(0, 0, BANK, "scalar")
-        angles(2, {})
-        sines(1)
-        angles(3, {})
-        sines(2)
-        join(1, 0, BANK, "scalar")
-        sines(3)
-        join(0, BANK, BANK, "vector")
-        roots(0, BANK, squares(0, BANK, 6))
-        first_bank = 2
+        planar = maxima(0, 0, BANK)
+        turned_group(2)
+        place(4)
+        place(5)
+        for i in range(4, 8):
+            angle(i)
+            wrap(i)
+        place(6)
+        place(7)
+        weave(0, 0, BANK, planar, "scalar")
+        turned_group(3)
+        weave(1, 0, BANK, maxima(1, 0, BANK), "vector")
+        nc.scalar.activation(warm[:], turns[1, 1][:, 3, BANK - 1 : BANK], ACT.Sqrt, bias=one[:], scale=0.0)
+        finish(0, BANK, unit_bank[4:8], big("score")[:].rearrange("p n j -> p (n j)"))
+        weave(0, BANK, BANK, maxima(0, BANK, BANK), "vector")
+        first_bank = 0
         for c0, width in PIECES:
-            join(1, c0, width, "vector")
-            roots(c0, width, squares(c0, width, first_bank))
-            first_bank += 4 * width // BANK
+            weave(1, c0, width, maxima(1, c0, width), "vector")
+            n_banks = 4 * width // BANK
+            score = keep.tile([P, 4 * width], F32, name="score%d" % c0)
+            finish(c0, width, [banks[i] for i in (2, 3, 6, 7)][first_bank : first_bank + n_banks], score[:])
+            first_bank += n_banks

@@ -54,7 +54,7 @@ def tile_list_slate_splitting_scores_kernel(
         w2s = held("w2s", [P, H], U8)
         w3w = held("w3w", [P, 2, N], I32)
         w3s = held("w3s", [P, N], U8)
-        wg = held("wg", [P, PACK * SP], F32)
+        wg = [held("wg%d" % t, [P, SP], F32) for t in range(PACK)]
         ga_t = held("ga_t", [P, 2, PACK], F32)
         gr = [keep.tile([P, SP], F32, name="gr%d" % k, tag="slice%d" % (k + 1 if k >= 3 else -k - 1)) for k in range(8)]
         pages = {}
@@ -113,19 +113,19 @@ def tile_list_slate_splitting_scores_kernel(
             rows = w1[a * KP : (a + 1) * KP, b * KP : (b + 1) * KP]
             nc.sync.dma_start(w1_raw[a, b][:], rows.rearrange("(p j) c -> p j c", j=PACK))
 
+        dealt = [keep.tile([P, BANK], F32, name="dealt%d" % jt, tag="late%d" % (4 + jt)) for jt in range(4)]
         nc.sync.dma_start(offs2_t[:], offs2)
         nc.sync.dma_start(w2w_raw[:].bitcast(I32), w2_words[0].bitcast(I32))
-        nc.sync.dma_start(pos_t[:], pos1)
+        wgs_raw = ring.tile([P, SP], F32, name="wgs_raw", tag="full", bufs=2)
+        nc.sync.dma_start(wgs_raw[:], wgs)
         load_scale_rows(w2s_raw, w2_scales, 0)
         load_words(tab2w[:], tab2_words[0])
         load_scale_rows(tab2s, tab2_scales, 0)
         load_grain(0)
-        wgs_v = wgs.rearrange("(m t) j -> m (t j)", t=PACK)
-        for q in (0, 2, 1, 3):
-            nc.sync.dma_start(wg[32 * q : 32 * q + 32, :], wgs_v)
+        nc.sync.dma_start(pos_t[:], pos1)
         load_grain(1)
-        load_words(tabw[0][:], tab_words[0])
         load_packed_rows(tabs, tab_scales)
+        load_words(tabw[0][:], tab_words[0])
         nc.sync.dma_start(offs_t[:], offs)
         load_w1(0, 0)
         load_w1(1, 0)
@@ -140,13 +140,27 @@ def tile_list_slate_splitting_scores_kernel(
         nc.sync.dma_start(w3w[:], w3_words.rearrange("a p n i -> p a (n i)").bitcast(I32))
         load_packed_rows(w3s, w3_scales)
 
+        for jt in range(4):
+            nc.tensor.transpose(banks[2][:, jt * P : (jt + 1) * P], wgs_raw[:, jt * P : (jt + 1) * P], ident[:])
+        for jt in range(4):
+            rows = banks[2][:, jt * P : (jt + 1) * P].rearrange("p (m t) -> p t m", t=PACK)
+            nc.scalar.copy(
+                dealt[jt][:].rearrange("p (t q m) -> p t q m", t=PACK, q=4),
+                rows.unsqueeze(2).to_broadcast([P, PACK, 4, 32]),
+            )
+        for t in range(PACK):
+            bank = banks[3 - t % 2]
+            for jt in range(4):
+                nc.tensor.transpose(bank[:, jt * P : (jt + 1) * P], dealt[jt][:, t * P : (t + 1) * P], ident[:])
+            nc.scalar.copy(wg[t][:], bank[:])
+
         nc.vector.tensor_copy(
-            w2w[:].bitcast(U16).rearrange("p (b t m) -> p b t m", b=2, t=PACK),
-            w2w_raw[:].bitcast(U16).rearrange("p (b m t) -> p b t m", b=2, t=PACK),
+            w2w[:].bitcast(U16).rearrange("p (b t g m) -> p b g t m", b=2, t=PACK, m=8),
+            w2w_raw[:].bitcast(U16).rearrange("p (b g m t) -> p b g t m", b=2, t=PACK, m=8),
         )
         nc.vector.tensor_copy(
-            w2s[:].rearrange("p (b t m) -> p b t m", b=2, t=PACK),
-            w2s_raw[:].rearrange("p (b m t) -> p b t m", b=2, t=PACK),
+            w2s[:].rearrange("p (b t g m) -> p b g t m", b=2, t=PACK, m=16),
+            w2s_raw[:].rearrange("p (b g m t) -> p b g t m", b=2, t=PACK, m=16),
         )
         nc.vector.tensor_copy(g2w[:], tab2w[:].bitcast(U32).indirect(offs2_t[:]))
         nc.vector.tensor_copy(g2s[:], tab2s[:].indirect(offs2_t[:]))
@@ -174,13 +188,13 @@ def tile_list_slate_splitting_scores_kernel(
             if 4 <= k + 1 < 8:
                 clear_page(k + 1)
             t = k % PACK
-            nc.vector.tensor_tensor(pages[k][:].indirect(pos_t[:]), bsum[:], wg[:, t * SP : (t + 1) * SP], ALU.mult)
+            nc.vector.tensor_tensor(pages[k][:].indirect(pos_t[:]), bsum[:], wg[t][:], ALU.mult)
 
         def quantise_w1(a, b):
             w1_bf = ring.tile([P, PACK * KP], BF16, name="w1_bf", tag="woven512", align_bytes=64)
             nc.scalar.copy(
-                w1_bf[:].rearrange("p (t m j) -> p m j t", t=PACK, j=PACK),
-                w1_raw[a, b][:].rearrange("p j (m t) -> p m j t", t=PACK),
+                w1_bf[:].rearrange("p (t m j) -> p m t j", t=PACK, j=PACK),
+                w1_raw[a, b][:].rearrange("p j (m t) -> p m t j", t=PACK),
             )
             nc.vector.quantize_mx(w1c[a][b][:].bitcast(FP8X4), w1s[a][b][:], w1_bf[:])
 
@@ -248,8 +262,8 @@ def tile_list_slate_splitting_scores_kernel(
             back = banks[6 + i % 2]
             for t in range(PACK):
                 cols = slice(t * P, (t + 1) * P)
-                nc.tensor.matmul(back[:, cols], lhsT=full[:, cols], rhs=ident[:], start=True, stop=False, is_transpose=True)
-                nc.tensor.matmul(back[:, cols], lhsT=minus[:, cols], rhs=ident[:], start=False, stop=True, is_transpose=True)
+                nc.tensor.matmul(back[:, cols], lhsT=minus[:, cols], rhs=ident[:], start=True, stop=False, is_transpose=True)
+                nc.tensor.matmul(back[:, cols], lhsT=full[:, cols], rhs=ident[:], start=False, stop=True, is_transpose=True)
             parts[i] = back
 
         def sine_turned(i):

@@ -61,7 +61,8 @@ def tile_list_slate_splitting_scores_kernel(
 
         def clear_page(k):
             pages[k] = keep.tile([P, S], F32, name="page%d" % k, tag="slice%d" % k)
-            nc.vector.memset(pages[k][:].bitcast(I32), 0)
+            engine = nc.vector if k < 4 else nc.gpsimd
+            engine.memset(pages[k][:].bitcast(I32), 0)
 
         gw = [[held("gw%d%d" % (a, h), [P, BANK], U32) for h in range(2)] for a in range(2)]
         gs = held("gs", [P, S], U8)
@@ -69,7 +70,7 @@ def tile_list_slate_splitting_scores_kernel(
         g2s = held("g2s", [P, SP], U8)
         w1c = [[held("w1c%d%d" % (a, b), [P, KP], U32) for b in range(2)] for a in range(2)]
         w1s = [[held("w1s%d%d" % (a, b), [P, KP], U8) for b in range(2)] for a in range(2)]
-        zc = [[held("zc%d%d" % (b, h), [P, BANK], U32) for h in range(2)] for b in range(2)]
+        zc = {(b, h): held("zc%d%d" % (b, h), [P, BANK], U32) for b, h in ((0, 0), (0, 1), (1, 1))}
         zs = [[held("zs%d%d" % (b, h), [P, BANK], U8) for h in range(2)] for b in range(2)]
         one = held("one", [P, 1], F32)
         warm = held("warm", [P, 1], F32)
@@ -113,7 +114,7 @@ def tile_list_slate_splitting_scores_kernel(
             rows = w1[a * KP : (a + 1) * KP, b * KP : (b + 1) * KP]
             nc.sync.dma_start(w1_raw[a, b][:], rows.rearrange("(p j) c -> p j c", j=PACK))
 
-        dealt = [keep.tile([P, BANK], F32, name="dealt%d" % jt, tag="late%d" % (4 + jt)) for jt in range(4)]
+        dealt = [keep.tile([P, BANK], F32, name="dealt%d" % jt, tag="late%d" % (4 + jt), align_bytes=64) for jt in range(4)]
         nc.sync.dma_start(offs2_t[:], offs2)
         nc.sync.dma_start(w2w_raw[:].bitcast(I32), w2_words[0].bitcast(I32))
         wgs_raw = ring.tile([P, SP], F32, name="wgs_raw", tag="full", bufs=2)
@@ -166,11 +167,11 @@ def tile_list_slate_splitting_scores_kernel(
         nc.vector.tensor_copy(g2s[:], tab2s[:].indirect(offs2_t[:]))
 
         unit_bank = [banks[i] for i in (6, 7, 6, 7, 0, 1, 4, 5)]
-        late = {8: 4, 9: 5, 6: 6, 7: 7}
+        late = {9: 4, 10: 5, 11: 6, 4: 7, 15: 8}
 
         def whole_tile(i):
             if i in late:
-                return keep.tile([P, BANK], U32, name="whole", tag="late%d" % late[i])
+                return keep.tile([P, BANK], U32, name="whole", tag="late%d" % late[i], align_bytes=64)
             return ring.tile([P, BANK], U32, name="whole", tag="whole", bufs=4)
 
         def place(k):
@@ -183,16 +184,16 @@ def tile_list_slate_splitting_scores_kernel(
             if k < 4:
                 bsum = ring.tile([P, SP], F32, name="bsum", tag="bsum")
             else:
-                bsum = keep.tile([P, SP], F32, name="bsum", tag="late%d" % k)
+                bsum = keep.tile([P, SP], F32, name="bsum", tag="late%d" % k, align_bytes=64)
             nc.vector.tensor_tensor(bsum[:], bank[:], gr[k][:], ALU.add)
             if 4 <= k + 1 < 8:
                 clear_page(k + 1)
             t = k % PACK
             nc.vector.tensor_tensor(pages[k][:].indirect(pos_t[:]), bsum[:], wg[t][:], ALU.mult)
 
-        def quantise_w1(a, b):
+        def quantise_w1(a, b, copy):
             w1_bf = ring.tile([P, PACK * KP], BF16, name="w1_bf", tag="woven512", align_bytes=64)
-            nc.scalar.copy(
+            copy(
                 w1_bf[:].rearrange("p (t m j) -> p m t j", t=PACK, j=PACK),
                 w1_raw[a, b][:].rearrange("p j (m t) -> p m t j", t=PACK),
             )
@@ -206,9 +207,9 @@ def tile_list_slate_splitting_scores_kernel(
         place(1)
         gather_words(0, 0)
         nc.vector.tensor_copy(gs[:], tabs[:].indirect(offs_t[:]))
-        quantise_w1(0, 0)
+        quantise_w1(0, 0, nc.scalar.copy)
         gather_words(0, 1)
-        quantise_w1(1, 0)
+        quantise_w1(1, 0, nc.scalar.copy)
         gather_words(1, 0)
         gather_words(1, 1)
         place(2)
@@ -241,15 +242,15 @@ def tile_list_slate_splitting_scores_kernel(
 
         parts = {}
 
-        def angle_turned(i):
-            b, jt = i // 4 % 2, i % 4
+        def angle_turned(i, earlier):
+            h, b, jt = i // 8, i // 4 % 2, i % 4
             if jt == 0:
-                turns[b, 1] = big("turns%d1" % b)
+                turns[b, h] = big("turns%d%d" % (b, h))
             bank = banks[2 + i % 2]
             for a in range(2):
                 nc.tensor.matmul_mx(
-                    bank[:], lhsT=gw[a][1][:, jt * P : (jt + 1) * P].bitcast(FP8X4),
-                    lhsT_scale=gs[4 * a : P, BANK + jt * P : BANK + (jt + 1) * P],
+                    bank[:], lhsT=gw[a][h][:, jt * P : (jt + 1) * P].bitcast(FP8X4),
+                    lhsT_scale=gs[4 * a : P, h * BANK + jt * P : h * BANK + (jt + 1) * P],
                     rhs=w1c[a][b][:].bitcast(FP8X4), rhs_scale=w1s[a][b][:],
                     start=(a == 0), stop=(a == 1),
                 )
@@ -257,6 +258,8 @@ def tile_list_slate_splitting_scores_kernel(
             full = ring.tile([P, BANK], F32, name="full", tag="full", bufs=2)
             minus = ring.tile([P, BANK], F32, name="minus", tag="minus", bufs=2)
             nc.scalar.activation(whole[:], bank[:], ACT.Copy, scale=0.5 / math.pi, bias=ROUND)
+            if earlier is not None:
+                sine_turned(earlier)
             nc.scalar.activation(full[:], bank[:], ACT.Copy, scale=0.5 / math.pi)
             nc.scalar.activation(minus[:], whole[:], ACT.Copy, scale=-1.0, bias=ROUND)
             back = banks[6 + i % 2]
@@ -267,9 +270,9 @@ def tile_list_slate_splitting_scores_kernel(
             parts[i] = back
 
         def sine_turned(i):
-            b, jt = i // 4 % 2, i % 4
+            h, b, jt = i // 8, i // 4 % 2, i % 4
             nc.scalar.activation(
-                turns[b, 1][:, :, jt * P : (jt + 1) * P], parts[i][:].rearrange("p (t j) -> p t j", t=PACK),
+                turns[b, h][:, :, jt * P : (jt + 1) * P], parts[i][:].rearrange("p (t j) -> p t j", t=PACK),
                 ACT.Sin, scale=2.0 * math.pi,
             )
 
@@ -280,7 +283,10 @@ def tile_list_slate_splitting_scores_kernel(
 
         def maxima(b, c0, width):
             h, lo = divmod(c0, BANK)
-            planar = ring.tile([P, PACK, width], BF16, name="planar", tag="planar%d" % width, bufs=1 if width == BANK else 2, align_bytes=64)
+            if (b, c0) == (0, BANK):
+                planar = keep.tile([P, PACK, width], BF16, name="planar", tag="late9", align_bytes=64)
+            else:
+                planar = ring.tile([P, PACK, width], BF16, name="planar", tag="planar%d" % width, bufs=1 if width == BANK else 2, align_bytes=64)
             for t in range(PACK):
                 nc.vector.scalar_tensor_tensor(
                     planar[:, t, :], turns[b, h][:, t, lo : lo + width], ga_t[:, b, t : t + 1],
@@ -288,16 +294,16 @@ def tile_list_slate_splitting_scores_kernel(
                 )
             return planar
 
-        def weave(b, c0, width, planar, engine):
+        def weave(b, c0, width, planar):
             h, lo = divmod(c0, BANK)
-            woven = ring.tile([P, width * PACK], BF16, name="woven", tag="woven%d" % width, align_bytes=64)
-            dst = woven[:].rearrange("p (c i t) -> p c t i", i=4, t=PACK)
-            src = planar[:].rearrange("p t (c i) -> p c t i", i=4)
-            if engine == "scalar":
-                nc.scalar.copy(dst, src)
+            if (b, c0) == (1, 0):
+                woven = keep.tile([P, width * PACK], BF16, name="woven", tag="late9", align_bytes=64)
             else:
-                nc.vector.tensor_copy(dst, src)
-            nc.vector.quantize_mx(zc[b][h][:, lo : lo + width].bitcast(FP8X4), zs[b][h][:, lo : lo + width], woven[:])
+                woven = ring.tile([P, width * PACK], BF16, name="woven", tag="woven%d" % width, align_bytes=64)
+            nc.vector.tensor_copy(
+                woven[:].rearrange("p (c i t) -> p c t i", i=4, t=PACK), planar[:].rearrange("p t (c i) -> p c t i", i=4)
+            )
+            nc.vector.quantize_mx(zc[b, h][:, lo : lo + width].bitcast(FP8X4), zs[b][h][:, lo : lo + width], woven[:])
 
         out_v = out.rearrange("(n p) j -> p n j", p=P)
 
@@ -313,7 +319,7 @@ def tile_list_slate_splitting_scores_kernel(
                         nc.tensor.matmul_mx(
                             bank[:, n * width : (n + 1) * width], lhsT=w3w[:, b, n0 : n0 + P].bitcast(FP8X4),
                             lhsT_scale=w3s[4 * b : P, n0 : n0 + P],
-                            rhs=zc[b][h][:, lo : lo + width].bitcast(FP8X4), rhs_scale=zs[b][h][:, lo : lo + width],
+                            rhs=zc[b, h][:, lo : lo + width].bitcast(FP8X4), rhs_scale=zs[b][h][:, lo : lo + width],
                             start=(b == 1), stop=(b == 0),
                         )
                 nc.scalar.activation(score[:, g * BANK : (g + 1) * BANK], bank[:], ACT.Square)
@@ -330,41 +336,42 @@ def tile_list_slate_splitting_scores_kernel(
             for i in range(4 * g, 4 * g + 4, 2):
                 sine(i)
 
-        def turned_group(g):
-            for i in range(4 * g, 4 * g + 5):
-                if i < 4 * g + 4:
-                    angle_turned(i)
-                if i == 14:
-                    sines(1)
-                if i > 4 * g:
-                    sine_turned(i - 1)
+        order = [8, 9, 10, 11, 4, 5, 6, 7, 12, 13, 14, 15]
+
+        def turned(units):
+            for i in units:
+                n = order.index(i)
+                angle_turned(i, order[n - 2] if n >= 2 else None)
 
         for i in range(4):
             angle(i)
             wrap(i)
         place(3)
-        quantise_w1(0, 1)
-        quantise_w1(1, 1)
+        quantise_w1(0, 1, nc.vector.tensor_copy)
+        quantise_w1(1, 1, nc.scalar.copy)
+        turned([8])
         sines(0)
         planar = maxima(0, 0, BANK)
-        turned_group(2)
+        turned([9, 10, 11])
         place(4)
         place(5)
-        for i in range(4, 8):
-            angle(i)
-            wrap(i)
+        weave(0, 0, BANK, planar)
+        turned([4, 5, 6, 7])
         place(6)
         place(7)
-        weave(0, 0, BANK, planar, "scalar")
-        turned_group(3)
-        weave(1, 0, BANK, maxima(1, 0, BANK), "vector")
+        turned([12, 13, 14, 15])
+        sine_turned(14)
+        sine_turned(15)
+        zc[1, 0] = keep.tile([P, BANK], U32, name="zc10", tag="late8", align_bytes=64)
+        weave(1, 0, BANK, maxima(1, 0, BANK))
         nc.scalar.activation(warm[:], turns[1, 1][:, 3, BANK - 1 : BANK], ACT.Sqrt, bias=one[:], scale=0.0)
         finish(0, BANK, unit_bank[4:8], big("score")[:].rearrange("p n j -> p (n j)"))
-        weave(0, BANK, BANK, maxima(0, BANK, BANK), "vector")
+        weave(0, BANK, BANK, maxima(0, BANK, BANK))
         first_bank = 0
         for c0, width in PIECES:
-            weave(1, c0, width, maxima(1, c0, width), "vector")
+            weave(1, c0, width, maxima(1, c0, width))
             n_banks = 4 * width // BANK
-            score = keep.tile([P, 4 * width], F32, name="score%d" % c0)
+            tag = "score" if n_banks == 2 else "late%d" % (2 + first_bank)
+            score = keep.tile([P, 4 * width], F32, name="score%d" % c0, tag=tag, align_bytes=64)
             finish(c0, width, [banks[i] for i in (2, 3, 6, 7)][first_bank : first_bank + n_banks], score[:])
             first_bank += n_banks

import math
from contextlib import ExitStack

import concourse.mybir as mybir
from concourse.masks import make_identity

K, K2, T, T2, S, SP, H, N = 1024, 512, 4096, 2048, 1024, 512, 1024, 512
FLOPS = 2 * (K * H * S + K2 * H * SP + H * N * S)

F32 = mybir.dt.float32
BF16 = mybir.dt.bfloat16
I32 = mybir.dt.int32
U32 = mybir.dt.uint32
U16 = mybir.dt.uint16
U8 = mybir.dt.uint8
FP8X4 = mybir.dt.float8_e4m3fn_x4
FP4X4 = mybir.dt.float4_e2m1fn_x4
ALU = mybir.AluOpType
ACT = mybir.ActivationFunctionType

P = 128
PACK = 4
KP = P * PACK
BANK = 512
ROUND = 1.5 * 2.0**23
PIECES = ((512, 256), (768, 128), (896, 128))


def tile_list_slate_splitting_scores_kernel(
    tc, tab_words, tab_scales, offs, tab2_words, tab2_scales, offs2, pos1,
    w1, ga, w2_words, w2_scales, grain, wgs, w3_words, w3_scales, out,
):
    nc = tc.nc
    with ExitStack() as ctx:
        keep = ctx.enter_context(tc.tile_pool(name="keep", bufs=1))
        ring = ctx.enter_context(tc.tile_pool(name="ring", bufs=2))
        psum = ctx.enter_context(tc.psum_pool(name="psum", bufs=1))

        def held(name, shape, dtype):
            return keep.tile(shape, dtype, name=name, align_bytes=64)

        banks = [psum.tile([P, BANK], F32, name="bank%d" % i) for i in range(8)]

        offs_t = keep.tile([P, S // 16], U16, name="offs_t")
        offs2_t = keep.tile([P, SP // 16], U16, name="offs2_t")
        pos_t = keep.tile([P, SP // 16], U16, name="pos_t")
        tabw = [held("tabw%d" % a, [P, T], I32) for a in range(2)]
        tabs = held("tabs", [P, T], U8)
        tab2w = held("tab2w", [P, T2], I32)
        tab2s = held("tab2s", [P, T2], U8)
        w2w_raw = held("w2w_raw", [P, 2 * H], U8)
        w2s_raw = held("w2s_raw", [P, H], U8)
        w2w = held("w2w", [P, 2 * H], U8)
        w2s = held("w2s", [P, H], U8)
        w3w = held("w3w", [P, 2, N], I32)
        w3s = held("w3s", [P, N], U8)
        wg = [held("wg%d" % t, [P, SP], F32) for t in range(PACK)]
        ga_t = held("ga_t", [P, 2, PACK], F32)
        gr = [keep.tile([P, SP], F32, name="gr%d" % k, tag="slice%d" % (k + 1 if k >= 3 else -k - 1)) for k in range(8)]
        pages = {}

        def clear_page(k):
            pages[k] = keep.tile([P, S], F32, name="page%d" % k, tag="slice%d" % k)
            engine = nc.vector if k < 4 else nc.gpsimd
            engine.memset(pages[k][:].bitcast(I32), 0)

        gw = [[held("gw%d%d" % (a, h), [P, BANK], U32) for h in range(2)] for a in range(2)]
        gs = held("gs", [P, S], U8)
        g2w = held("g2w", [P, SP], U32)
        g2s = held("g2s", [P, SP], U8)
        w1c = [[held("w1c%d%d" % (a, b), [P, KP], U32) for b in range(2)] for a in range(2)]
        w1s = [[held("w1s%d%d" % (a, b), [P, KP], U8) for b in range(2)] for a in range(2)]
        zc = {(b, h): held("zc%d%d" % (b, h), [P, BANK], U32) for b, h in ((0, 0), (0, 1), (1, 1))}
        zs = [[held("zs%d%d" % (b, h), [P, BANK], U8) for h in range(2)] for b in range(2)]
        one = held("one", [P, 1], F32)
        warm = held("warm", [P, 1], F32)

        def big(name):
            return ring.tile([P, PACK, BANK], F32, name=name, tag="big", bufs=5, align_bytes=64)

        nc.gpsimd.memset(w2s_raw[:].bitcast(I32), 0)
        nc.gpsimd.memset(tab2s[:].bitcast(I32), 0)
        nc.vector.memset(one[:], 1.0)
        nc.scalar.activation(warm[:], one[:], ACT.Sin)
        nc.vector.memset(tabs[:].bitcast(I32), 0)
        nc.vector.memset(w3s[:].bitcast(I32), 0)
        for k in range(4):
            clear_page(k)

        ident = held("ident", [P, P], F32)
        make_identity(nc, ident[:])

        def load_words(tile_ap, words):
            nc.sync.dma_start(tile_ap, words.rearrange("p n i -> p (n i)").bitcast(I32))

        def load_scale_rows(tile, scales, a):
            for q in range(4):
                r0 = 32 * q + 4 * a
                nc.sync.dma_start(tile[r0 : r0 + 4, :].bitcast(I32), scales[a, 4 * q : 4 * q + 4, :].bitcast(I32))

        def load_packed_rows(tile, scales):
            for q in range(4):
                nc.sync.dma_start(tile[32 * q : 32 * q + 8, :].bitcast(I32), scales[:, 4 * q : 4 * q + 4, :].bitcast(I32))

        grain_v = grain.rearrange("(b p t) j -> b t p j", b=2, t=PACK)

        def load_grain(k):
            nc.sync.dma_start(gr[k][:], grain_v[k // PACK, k % PACK])

        w1_raw = {}

        def load_w1(a, b):
            w1_raw[a, b] = big("w1_raw%d%d" % (a, b))
            rows = w1[a * KP : (a + 1) * KP, b * KP : (b + 1) * KP]
            nc.sync.dma_start(w1_raw[a, b][:], rows.rearrange("(p j) c -> p j c", j=PACK))

        dealt = [keep.tile([P, BANK], F32, name="dealt%d" % jt, tag="late%d" % (4 + jt), align_bytes=64) for jt in range(4)]
        nc.sync.dma_start(offs2_t[:], offs2)
        nc.sync.dma_start(w2w_raw[:].bitcast(I32), w2_words[0].bitcast(I32))
        wgs_raw = ring.tile([P, SP], F32, name="wgs_raw", tag="full", bufs=2)
        nc.sync.dma_start(wgs_raw[:], wgs)
        load_scale_rows(w2s_raw, w2_scales, 0)
        load_words(tab2w[:], tab2_words[0])
        load_scale_rows(tab2s, tab2_scales, 0)
        load_grain(0)
        nc.sync.dma_start(pos_t[:], pos1)
        load_grain(1)
        load_packed_rows(tabs, tab_scales)
        load_words(tabw[0][:], tab_words[0])
        nc.sync.dma_start(offs_t[:], offs)
        load_w1(0, 0)
        load_w1(1, 0)
        load_words(tabw[1][:], tab_words[1])
        load_grain(2)
        load_w1(0, 1)
        load_grain(3)
        load_w1(1, 1)
        nc.sync.dma_start(ga_t[:], ga.rearrange("(b p t) -> p b t", b=2, t=PACK))
        for k in range(4, 8):
            load_grain(k)
        nc.sync.dma_start(w3w[:], w3_words.rearrange("a p n i -> p a (n i)").bitcast(I32))
        load_packed_rows(w3s, w3_scales)

        for jt in range(4):
            nc.tensor.transpose(banks[2][:, jt * P : (jt + 1) * P], wgs_raw[:, jt * P : (jt + 1) * P], ident[:])
        for jt in range(4):
            rows = banks[2][:, jt * P : (jt + 1) * P].rearrange("p (m t) -> p t m", t=PACK)
            nc.scalar.copy(
                dealt[jt][:].rearrange("p (t q m) -> p t q m", t=PACK, q=4),
                rows.unsqueeze(2).to_broadcast([P, PACK, 4, 32]),
            )
        for t in range(PACK):
            bank = banks[3 - t % 2]
            for jt in range(4):
                nc.tensor.transpose(bank[:, jt * P : (jt + 1) * P], dealt[jt][:, t * P : (t + 1) * P], ident[:])
            nc.scalar.copy(wg[t][:], bank[:])

        nc.vector.tensor_copy(
            w2w[:].bitcast(U16).rearrange("p (b t g m) -> p b g t m", b=2, t=PACK, m=8),
            w2w_raw[:].bitcast(U16).rearrange("p (b g m t) -> p b g t m", b=2, t=PACK, m=8),
        )
        nc.vector.tensor_copy(
            w2s[:].rearrange("p (b t g m) -> p b g t m", b=2, t=PACK, m=16),
            w2s_raw[:].rearrange("p (b g m t) -> p b g t m", b=2, t=PACK, m=16),
        )
        nc.vector.tensor_copy(g2w[:], tab2w[:].bitcast(U32).indirect(offs2_t[:]))
        nc.vector.tensor_copy(g2s[:], tab2s[:].indirect(offs2_t[:]))

        unit_bank = [banks[i] for i in (6, 7, 6, 7, 0, 1, 4, 5)]
        late = {9: 4, 10: 5, 11: 6, 4: 7, 15: 8}

        def whole_tile(i):
            if i in late:
                return keep.tile([P, BANK], U32, name="whole", tag="late%d" % late[i], align_bytes=64)
            return ring.tile([P, BANK], U32, name="whole", tag="whole", bufs=4)

        def place(k):
            c0 = P * k
            bank = unit_bank[k]
            nc.tensor.matmul_mx(
                bank[:], lhsT=w2w[:, 2 * c0 : 2 * c0 + 2 * P].bitcast(FP4X4), lhsT_scale=w2s[:, c0 : c0 + P],
                rhs=g2w[:].bitcast(FP8X4), rhs_scale=g2s[:], start=True, stop=True,
            )
            if k < 4:
                bsum = ring.tile([P, SP], F32, name="bsum", tag="bsum")
            else:
                bsum = keep.tile([P, SP], F32, name="bsum", tag="late%d" % k, align_bytes=64)
            nc.vector.tensor_tensor(bsum[:], bank[:], gr[k][:], ALU.add)
            if 4 <= k + 1 < 8:
                clear_page(k + 1)
            t = k % PACK
            nc.vector.tensor_tensor(pages[k][:].indirect(pos_t[:]), bsum[:], wg[t][:], ALU.mult)

        def quantise_w1(a, b, copy):
            w1_bf = ring.tile([P, PACK * KP], BF16, name="w1_bf", tag="woven512", align_bytes=64)
            copy(
                w1_bf[:].rearrange("p (t m j) -> p m t j", t=PACK, j=PACK),
                w1_raw[a, b][:].rearrange("p j (m t) -> p m t j", t=PACK),
            )
            nc.vector.quantize_mx(w1c[a][b][:].bitcast(FP8X4), w1s[a][b][:], w1_bf[:])

        def gather_words(a, h):
            part = offs_t[:, h * (BANK // 16) : (h + 1) * (BANK // 16)]
            nc.vector.tensor_copy(gw[a][h][:], tabw[a][:].bitcast(U32).indirect(part))

        place(0)
        place(1)
        gather_words(0, 0)
        nc.vector.tensor_copy(gs[:], tabs[:].indirect(offs_t[:]))
        quantise_w1(0, 0, nc.scalar.copy)
        gather_words(0, 1)
        quantise_w1(1, 0, nc.scalar.copy)
        gather_words(1, 0)
        gather_words(1, 1)
        place(2)

        turns = {}
        wholes = {}

        def angle(i):
            h, b, t = i // 8, i // 4 % 2, i % 4
            if t == 0:
                turns[b, h] = big("turns%d%d" % (b, h))
            bank = banks[2 + i % 2]
            for a in range(2):
                nc.tensor.matmul_mx(
                    bank[:], lhsT=w1c[a][b][:, t * P : (t + 1) * P].bitcast(FP8X4),
                    lhsT_scale=w1s[a][b][:, t * P : (t + 1) * P],
                    rhs=gw[a][h][:].bitcast(FP8X4), rhs_scale=gs[4 * a : P, h * BANK : (h + 1) * BANK],
                    start=(a == 0), stop=(a == 1),
                )
            whole = whole_tile(i)
            x = turns[b, h][:, t, :]
            nc.scalar.activation(x, bank[:], ACT.Copy, scale=0.5 / math.pi)
            nc.scalar.activation(whole[:], bank[:], ACT.Copy, scale=0.5 / math.pi, bias=ROUND)
            wholes[i] = whole

        def wrap(i):
            h, b, t = i // 8, i // 4 % 2, i % 4
            x = turns[b, h][:, t, :]
            nc.vector.scalar_tensor_tensor(x, wholes[i][:].bitcast(I32), ROUND, x, ALU.subtract, ALU.subtract)

        parts = {}

        def angle_turned(i, earlier):
            h, b, jt = i // 8, i // 4 % 2, i % 4
            if jt == 0:
                turns[b, h] = big("turns%d%d" % (b, h))
            bank = banks[2 + i % 2]
            for a in range(2):
                nc.tensor.matmul_mx(
                    bank[:], lhsT=gw[a][h][:, jt * P : (jt + 1) * P].bitcast(FP8X4),
                    lhsT_scale=gs[4 * a : P, h * BANK + jt * P : h * BANK + (jt + 1) * P],
                    rhs=w1c[a][b][:].bitcast(FP8X4), rhs_scale=w1s[a][b][:],
                    start=(a == 0), stop=(a == 1),
                )
            whole = whole_tile(i)
            full = ring.tile([P, BANK], F32, name="full", tag="full", bufs=2)
            minus = ring.tile([P, BANK], F32, name="minus", tag="minus", bufs=2)
            nc.scalar.activation(whole[:], bank[:], ACT.Copy, scale=0.5 / math.pi, bias=ROUND)
            if earlier is not None:
                sine_turned(earlier)
            nc.scalar.activation(full[:], bank[:], ACT.Copy, scale=0.5 / math.pi)
            nc.scalar.activation(minus[:], whole[:], ACT.Copy, scale=-1.0, bias=ROUND)
            back = banks[6 + i % 2]
            for t in range(PACK):
                cols = slice(t * P, (t + 1) * P)
                nc.tensor.matmul(back[:, cols], lhsT=minus[:, cols], rhs=ident[:], start=True, stop=False, is_transpose=True)
                nc.tensor.matmul(back[:, cols], lhsT=full[:, cols], rhs=ident[:], start=False, stop=True, is_transpose=True)
            parts[i] = back

        def sine_turned(i):
            h, b, jt = i // 8, i // 4 % 2, i % 4
            nc.scalar.activation(
                turns[b, h][:, :, jt * P : (jt + 1) * P], parts[i][:].rearrange("p (t j) -> p t j", t=PACK),
                ACT.Sin, scale=2.0 * math.pi,
            )

        def sine(i):
            h, b, t = i // 8, i // 4 % 2, i % 4
            x = turns[b, h][:, t : t + 2, :]
            nc.scalar.activation(x, x, ACT.Sin, scale=-2.0 * math.pi)

        def maxima(b, c0, width):
            h, lo = divmod(c0, BANK)
            if (b, c0) == (0, BANK):
                planar = keep.tile([P, PACK, width], BF16, name="planar", tag="late9", align_bytes=64)
            else:
                planar = ring.tile([P, PACK, width], BF16, name="planar", tag="planar%d" % width, bufs=1 if width == BANK else 2, align_bytes=64)
            for t in range(PACK):
                nc.vector.scalar_tensor_tensor(
                    planar[:, t, :], turns[b, h][:, t, lo : lo + width], ga_t[:, b, t : t + 1],
                    pages[PACK * b + t][:, c0 : c0 + width], ALU.mult, ALU.max,
                )
            return planar

        def weave(b, c0, width, planar):
            h, lo = divmod(c0, BANK)
            if (b, c0) == (1, 0):
                woven = keep.tile([P, width * PACK], BF16, name="woven", tag="late9", align_bytes=64)
            else:
                woven = ring.tile([P, width * PACK], BF16, name="woven", tag="woven%d" % width, align_bytes=64)
            nc.vector.tensor_copy(
                woven[:].rearrange("p (c i t) -> p c t i", i=4, t=PACK), planar[:].rearrange("p t (c i) -> p c t i", i=4)
            )
            nc.vector.quantize_mx(zc[b, h][:, lo : lo + width].bitcast(FP8X4), zs[b][h][:, lo : lo + width], woven[:])

        out_v = out.rearrange("(n p) j -> p n j", p=P)

        def finish(c0, width, free_banks, score):
            h, lo = divmod(c0, BANK)
            per_bank = BANK // width
            n_banks = 4 // per_bank
            for g in range(n_banks):
                bank = free_banks[g % len(free_banks)]
                for n in range(per_bank):
                    n0 = (g * per_bank + n) * P
                    for b in (1, 0):
                        nc.tensor.matmul_mx(
                            bank[:, n * width : (n + 1) * width], lhsT=w3w[:, b, n0 : n0 + P].bitcast(FP8X4),
                            lhsT_scale=w3s[4 * b : P, n0 : n0 + P],
                            rhs=zc[b, h][:, lo : lo + width].bitcast(FP8X4), rhs_scale=zs[b][h][:, lo : lo + width],
                            start=(b == 1), stop=(b == 0),
                        )
                nc.scalar.activation(score[:, g * BANK : (g + 1) * BANK], bank[:], ACT.Square)
            step = min(2, n_banks)
            for g in range(0, n_banks, step):
                part = score[:, g * BANK : (g + step) * BANK]
                nc.scalar.activation(part, part, ACT.Sqrt, bias=one[:])
                nc.sync.dma_start(
                    out_v[:, g * per_bank : (g + step) * per_bank, c0 : c0 + width],
                    part.rearrange("p (n j) -> p n j", j=width),
                )

        def sines(g):
            for i in range(4 * g, 4 * g + 4, 2):
                sine(i)

        order = [8, 9, 10, 11, 4, 5, 6, 7, 12, 13, 14, 15]

        def turned(units):
            for i in units:
                n = order.index(i)
                angle_turned(i, order[n - 2] if n >= 2 else None)

        for i in range(4):
            angle(i)
            wrap(i)
        place(3)
        quantise_w1(0, 1, nc.vector.tensor_copy)
        quantise_w1(1, 1, nc.scalar.copy)
        turned([8])
        sines(0)
        planar = maxima(0, 0, BANK)
        turned([9, 10, 11])
        place(4)
        place(5)
        weave(0, 0, BANK, planar)
        turned([4, 5, 6, 7])
        place(6)
        place(7)
        turned([12, 13, 14, 15])
        sine_turned(14)
        sine_turned(15)
        zc[1, 0] = keep.tile([P, BANK], U32, name="zc10", tag="late8", align_bytes=64)
        weave(1, 0, BANK, maxima(1, 0, BANK))
        nc.scalar.activation(warm[:], turns[1, 1][:, 3, BANK - 1 : BANK], ACT.Sqrt, bias=one[:], scale=0.0)
        finish(0, BANK, unit_bank[4:8], big("score")[:].rearrange("p n j -> p (n j)"))
        weave(0, BANK, BANK, maxima(0, BANK, BANK))
        first_bank = 0
        for c0, width in PIECES:
            weave(1, c0, width, maxima(1, c0, width))
            n_banks = 4 * width // BANK
            tag = "score" if n_banks == 2 else "late%d" % (2 + first_bank)
            score = keep.tile([P, 4 * width], F32, name="score%d" % c0, tag=tag, align_bytes=64)
            finish(c0, width, [banks[i] for i in (2, 3, 6, 7)][first_bank : first_bank + n_banks], score[:])
            first_bank += n_banks
